import numpy as np
import ml_dtypes


def mxq(x, axis, fmt="e4m3"):
    dtype, down = {"e4m3": (ml_dtypes.float8_e4m3fn, 7), "e5m2": (ml_dtypes.float8_e5m2, 14)}[fmt]
    v = np.moveaxis(np.asarray(x, np.float32).astype(ml_dtypes.bfloat16).astype(np.float64), axis, -1)
    blocks = v.reshape(v.shape[:-1] + (-1, 32))
    amax = np.abs(blocks).max(-1, keepdims=True)
    byte = np.maximum(np.where(amax > 0, np.frexp(amax)[1] - 1 + 127, 0) - down, 1)
    scale = np.exp2(byte - 127.0)
    codes = (blocks / scale).astype(np.float32).astype(dtype).astype(np.float64)
    return np.moveaxis((codes * scale).reshape(v.shape), -1, axis)


WIDE = False


def mx_kscale(k):
    if not WIDE:
        return np.ones(k)
    levels = np.array([10, -10, 5, -5, 0])
    if k % 512:
        return np.exp2(np.random.permutation(np.resize(levels, k // 32))).repeat(32)
    a = np.empty((k // 512, 16))
    for p in range(k // 512):
        a[p, :8] = np.random.permutation(np.resize(levels, 8))
        for g in range(8):
            far = levels[np.abs(levels - a[p, g]) >= 10]
            a[p, g + 8] = far[np.random.randint(len(far))]
    return np.exp2(a.ravel()).repeat(32)


def f64(x):
    return np.asarray(x).astype(np.float64)


def striped(idx):
    return np.tile(idx.reshape(-1, 16).T, (8, 1)).astype(np.uint16)


def unstriped(offs):
    return offs[:16].T.reshape(-1).astype(np.int64)


E2M1 = np.array([0.0, 0.5, 1.0, 1.5, 2.0, 3.0, 4.0, 6.0, -0.0, -0.5, -1.0, -1.5, -2.0, -3.0, -4.0, -6.0])


def pack_weight(w, fmt):
    k, n = w.shape
    w = f64(np.asarray(w, np.float32).astype(ml_dtypes.bfloat16)).reshape(k // 32, 32, n)
    amax = np.abs(w).max(1)
    if fmt == "e4m3":
        byte = np.frexp(amax)[1] - 1 + 127 - 7
    else:
        mant, ex = np.frexp(amax / 6.0)
        byte = np.where(mant > 0.5, ex, ex - 1) + 127
    byte = np.clip(np.where(amax > 0, byte, 1), 1, 254)
    scaled = (w * np.exp2(127.0 - byte)[:, None, :]).reshape(k, n).astype(np.float32)
    by_word = np.ascontiguousarray(scaled.reshape(k // 512, 128, 4, n).transpose(0, 1, 3, 2))
    if fmt == "e4m3":
        words = by_word.astype(ml_dtypes.float8_e4m3fn).view(np.uint8)
    else:
        c = by_word.astype(ml_dtypes.float4_e2m1fn).view(np.uint8) & 0xF
        words = (c[..., 0::2] | (c[..., 1::2] << 4)).reshape(k // 512, 128, 2 * n)
    return np.ascontiguousarray(words), np.ascontiguousarray(byte.astype(np.uint8).reshape(k // 512, 16, n))


def unpack_weight(words, scales, fmt):
    g, _, n = scales.shape
    words = np.ascontiguousarray(words).reshape(g, 128, n, -1)
    if fmt == "e4m3":
        vals = words.view(ml_dtypes.float8_e4m3fn).astype(np.float64)
    else:
        nib = np.empty((g, 128, n, 4), np.uint8)
        nib[..., 0::2] = words & 0xF
        nib[..., 1::2] = words >> 4
        vals = E2M1[nib]
    vals = vals * np.repeat(np.exp2(scales.astype(np.float64) - 127.0), 8, axis=1)[..., None]
    return vals.transpose(0, 1, 3, 2).reshape(g * 512, n)


def gelu(v):
    return 0.5 * v * (1.0 + np.tanh(np.sqrt(2.0 / np.pi) * (v + 0.044715 * v**3)))


K, T, E, C, H, N = 1024, 768, 8, 128, 512, 256
TOP = 3
PAD = 64


def by_expert(wq, xq):
    return np.concatenate([wq[e].T @ xq[:, e * C:(e + 1) * C] for e in range(E)], axis=1)


def setup_inputs():
    n = np.random.standard_normal
    s = mx_kscale(K)[:, None]
    u = mx_kscale(H)
    slot_token = np.empty(E * C, np.int64); pos = np.tile(E * C + np.arange(T) % PAD, (TOP, 1)); taken = np.zeros(T, np.int64)
    liked = np.random.randn(T)
    for e in np.random.permutation(E):
        free = np.flatnonzero(taken < TOP); pick = np.random.permutation(free[np.argsort(-(liked[free] + np.random.gumbel(size=free.size)))[:C]]); slot_token[e * C:(e + 1) * C] = pick
        pos[taken[pick], pick] = e * C + np.arange(C); taken[pick] += 1
    g = np.random.uniform(0.2, 0.8, (TOP, T))
    w1 = [pack_weight(m, "e2m1") for m in n((E, K, H)) / np.sqrt(K) / s[None] * u[None, None, :]]
    w2 = [pack_weight(m, "e2m1") for m in n((E, H, N)) / np.sqrt(H) / u[None, :, None]]
    return {
        "xT": (n((K, T)) * s).astype(np.float32),
        "w1_words": np.stack([m[0] for m in w1]),
        "w1_scales": np.stack([m[1] for m in w1]),
        "w2_words": np.stack([m[0] for m in w2]),
        "w2_scales": np.stack([m[1] for m in w2]),
        "gate": np.stack([np.tile(r, (N, 1)) for r in g]).astype(np.float32),
        "offs": striped(slot_token),
        "pos1": striped(pos[0]),
        "pos2": striped(pos[1]),
        "pos3": striped(pos[2]),
    }


def reference(xT, w1_words, w1_scales, w2_words, w2_scales, gate, offs, pos1, pos2, pos3):
    idx = unstriped(offs)
    w1 = np.stack([unpack_weight(w1_words[e], w1_scales[e], "e2m1") for e in range(E)])
    w2 = np.stack([unpack_weight(w2_words[e], w2_scales[e], "e2m1") for e in range(E)])
    xq = mxq(f64(xT)[:, idx], 0, "e4m3")
    h = gelu(by_expert(w1, xq))
    y = by_expert(w2, mxq(h, 0, "e4m3"))
    y = np.concatenate([y, np.zeros((N, PAD))], axis=1)
    return sum(f64(gate[r]) * y[:, unstriped(p)] for r, p in enumerate((pos1, pos2, pos3)))

@@ -1,0 +1,255 @@
+from contextlib import ExitStack
+
+import concourse.mybir as mybir
+from concourse.masks import make_identity
+
+K, T, E, C, H, N = 1024, 768, 8, 128, 512, 256
+TOP = 3
+PAD = 64
+SLOTS = E * C
+FLOPS = 2 * SLOTS * (K * H + H * N)
+
+F32 = mybir.dt.float32
+BF16 = mybir.dt.bfloat16
+I32 = mybir.dt.int32
+U32 = mybir.dt.uint32
+U16 = mybir.dt.uint16
+U8 = mybir.dt.uint8
+FP8X4 = mybir.dt.float8_e4m3fn_x4
+FP4X4 = mybir.dt.float4_e2m1fn_x4
+ACT = mybir.ActivationFunctionType
+ALU = mybir.AluOpType
+
+P = 128
+PACK = 4
+K_PASS = P * PACK
+PASSES = K // K_PASS
+TOKEN_CHUNK = 256
+CHUNKS = T // TOKEN_CHUNK
+PAIR = 2
+PAIRS = E // PAIR
+PAIR_SLOTS = PAIR * C
+N_TILES = N // P
+LIST_COL = 16
+COMBINE_PIECES = ((0, 0, 384), (0, 384, 768), (1, 0, 384), (1, 384, 640), (1, 640, 768))
+
+
+def tile_moe_ecr_mlp_gelu_kernel(tc, xT, w1_words, w1_scales, w2_words, w2_scales, gate, offs, pos1, pos2, pos3, out):
+    nc = tc.nc
+    with ExitStack() as ctx:
+        keep = ctx.enter_context(tc.tile_pool(name="keep", bufs=1))
+        psum = ctx.enter_context(tc.psum_pool(name="psum", bufs=1))
+
+        def held(shape, dtype, name):
+            return keep.tile(shape, dtype, name=name, align_bytes=64)
+
+        offs_sb = keep.tile([P, SLOTS // LIST_COL], U16, name="offs_sb")
+        pos_sb = [keep.tile([P, T // LIST_COL], U16, name=f"pos_sb{r}") for r in range(TOP)]
+        def streamed(shape, dtype, name):
+            return keep.tile(shape, dtype, name=name, tag="streamed", bufs=4, align_bytes=64)
+
+        x_first = streamed([P, PACK, T], F32, "x_first")
+        x_second = [streamed([P, PACK, TOKEN_CHUNK], F32, f"x_second{c}") for c in range(CHUNKS)]
+        x_raw = [[x_first[:, :, c * TOKEN_CHUNK:(c + 1) * TOKEN_CHUNK] for c in range(CHUNKS)], [t[:] for t in x_second]]
+        x_bf = [[held([P, TOKEN_CHUNK, PACK], BF16, f"x_bf{s}_{c}") for c in range(CHUNKS)] for s in range(PASSES)]
+        token_codes = [held([P, T], U32, f"token_codes{s}") for s in range(PASSES)]
+        token_scales = [held([P, T], U8, f"token_scales{s}") for s in range(PASSES)]
+        w1_plane = [held([P, E // 2 * PASSES, H], U8, f"w1_plane{h}") for h in range(2)]
+        w2_plane = held([P, E, N], U8, "w2_plane")
+        y_sb = [held([P, SLOTS + PAD], F32, f"y_sb{m}") for m in range(N_TILES)]
+        identity = held([P, P], F32, "identity")
+
+        nc.gpsimd.memset(w1_plane[0][:].rearrange("p a b -> p (a b)").bitcast(I32), 0)
+        for plane in (w2_plane, w1_plane[1]):
+            nc.vector.memset(plane[:].rearrange("p a b -> p (a b)").bitcast(I32), 0)
+        for plane in token_scales:
+            nc.vector.memset(plane[:].bitcast(I32), 0)
+        nc.vector.memset(y_sb[0][:, SLOTS:], 0.0)
+        nc.scalar.activation(y_sb[1][:, SLOTS:], y_sb[0][:, SLOTS:], ACT.Gelu_apprx_tanh)
+        make_identity(nc, identity[:])
+
+        def x_rows(s):
+            return xT[s * K_PASS:(s + 1) * K_PASS, :].rearrange("(p j) t -> p j t", j=PACK)
+
+        def load_plane(plane, scales):
+            rows = scales.rearrange("e s (q r) i -> r q (e s) i", r=4)
+            for r in range(4):
+                nc.sync.dma_start(plane[r:P:32, :, :].bitcast(I32), rows[r].bitcast(I32))
+
+        def load_words(dst, words):
+            nc.sync.dma_start(dst.bitcast(I32), words.rearrange("e s p b -> p (e s) b").bitcast(I32))
+
+        nc.sync.dma_start(x_first[:], x_rows(0))
+        nc.sync.dma_start(offs_sb[:], offs)
+        for c in range(CHUNKS):
+            nc.sync.dma_start(x_second[c][:], x_rows(1)[:, :, c * TOKEN_CHUNK:(c + 1) * TOKEN_CHUNK])
+        w1_first = held([P, 2 * PASSES, 2 * H], U8, "w1_first")
+        load_words(w1_first[:], w1_words[0:2])
+        load_plane(w1_plane[0], w1_scales[0:4])
+        load_plane(w2_plane, w2_scales)
+        load_plane(w1_plane[1], w1_scales[4:8])
+        for r, pos in enumerate((pos1, pos2, pos3)):
+            nc.sync.dma_start(pos_sb[r][:], pos)
+        def round_tokens(s, c):
+            src = x_raw[s][c].rearrange("p j (a i) -> p a j i", i=4)
+            dst = x_bf[s][c][:].rearrange("p (a i) j -> p a j i", i=4)
+            if s == 0 and c < 2:
+                nc.vector.tensor_copy(dst, src)
+            else:
+                nc.scalar.activation(dst, src, ACT.Copy)
+
+        def quantise_tokens(s, c):
+            cols = slice(c * TOKEN_CHUNK, (c + 1) * TOKEN_CHUNK)
+            nc.vector.quantize_mx(
+                out=token_codes[s][:, cols].bitcast(FP8X4),
+                scales=token_scales[s][:, cols],
+                in_=x_bf[s][c][:].rearrange("p t j -> p (t j)"),
+            )
+
+        slot_codes, slot_scales, h_rows, turned, h_bf, h_codes, h_scales, y_bank = {}, {}, {}, {}, {}, {}, {}, {}
+
+        def gather(s, e0, e1):
+            entries = offs_sb[:, e0 * C // LIST_COL:e1 * C // LIST_COL]
+            codes = held([P, (e1 - e0) * C], U32, f"slot_codes{s}_{e0}")
+            scales = held([P, (e1 - e0) * C], U8, f"slot_scales{s}_{e0}")
+            nc.vector.tensor_copy(codes[:], token_codes[s][:].indirect(entries))
+            nc.vector.tensor_copy(scales[:], token_scales[s][:].indirect(entries))
+            for e in range(e0, e1):
+                slot_codes[s, e] = codes[:, (e - e0) * C:(e - e0 + 1) * C]
+                slot_scales[s, e] = scales[:, (e - e0) * C:(e - e0 + 1) * C]
+
+        def first_layer(e):
+            a_bank = psum.tile([P, H], F32, name=f"a_bank{e}", tag="wide", bufs=4)
+            for s in range(PASSES):
+                nc.tensor.matmul_mx(
+                    out=a_bank[:],
+                    lhsT=slot_codes[s, e].bitcast(FP8X4),
+                    lhsT_scale=slot_scales[s, e],
+                    rhs=w1_codes[e][:, s, :].bitcast(FP4X4),
+                    rhs_scale=w1_plane[e // 4][:, (e % 4) * PASSES + s, :],
+                    start=(s == 0),
+                    stop=(s == PASSES - 1),
+                )
+            h_rows[e] = held([P, H], BF16, f"h_rows{e}")
+            nc.scalar.activation(
+                h_rows[e][:].rearrange("c (u m d) -> c u m d", u=2, d=2),
+                a_bank[:].rearrange("c (m u d) -> c u m d", u=2, d=2),
+                ACT.Gelu_apprx_tanh,
+            )
+
+        def turn(e0, e1, on_vector=False):
+            bank = psum.tile([P, e1 - e0, 2, C], F32, name=f"turned{e0}", tag="turned", bufs=2)
+            for e in range(e0, e1):
+                h_words = h_rows[e][:].bitcast(F32)
+                for u in range(2):
+                    nc.tensor.transpose(bank[:, e - e0, u, :], h_words[:, u * P:(u + 1) * P], identity[:])
+            h_bf[e0] = held([P, (e1 - e0) * C * PACK], BF16, f"h_bf{e0}")
+            dst = h_bf[e0][:].bitcast(F32).rearrange("p (j c u) -> p j c u", j=e1 - e0, u=2)
+            src = bank[:].rearrange("p j u c -> p j c u")
+            if on_vector:
+                nc.vector.tensor_copy(dst, src)
+            else:
+                nc.scalar.copy(dst, src)
+
+        def quantise_h(e0, e1):
+            codes = held([P, (e1 - e0) * C], U32, f"h_codes{e0}")
+            scales = held([P, (e1 - e0) * C], U8, f"h_scales{e0}")
+            nc.vector.quantize_mx(out=codes[:].bitcast(FP8X4), scales=scales[:], in_=h_bf[e0][:])
+            for e in range(e0, e1):
+                h_codes[e] = codes[:, (e - e0) * C:(e - e0 + 1) * C]
+                h_scales[e] = scales[:, (e - e0) * C:(e - e0 + 1) * C]
+
+        def second_layer(m, e0, e1):
+            for e in range(e0, e1):
+                if e % 4 == 0:
+                    tag, bufs = ("y_first", 2) if m == 0 else ("wide", 4)
+                    y_bank[m, e // 4] = psum.tile([P, 4 * C], F32, name=f"y_bank{m}_{e}", tag=tag, bufs=bufs)
+                nc.tensor.matmul_mx(
+                    out=y_bank[m, e // 4][:, (e % 4) * C:(e % 4 + 1) * C],
+                    lhsT=w2_codes[:, e, 2 * P * m:2 * P * (m + 1)].bitcast(FP4X4),
+                    lhsT_scale=w2_plane[:, e, P * m:P * (m + 1)],
+                    rhs=h_codes[e].bitcast(FP8X4),
+                    rhs_scale=h_scales[e],
+                    start=True,
+                    stop=True,
+                )
+
+        def leave_psum(m, e0, e1, on_vector=False):
+            dst = y_sb[m][:, e0 * C:e1 * C]
+            src = y_bank[m, e0 // 4][:, (e0 % 4) * C:(e0 % 4 + e1 - e0) * C]
+            if on_vector:
+                nc.vector.tensor_copy(dst, src)
+            else:
+                nc.scalar.copy(dst, src)
+
+        for c in (2, 0, 1):
+            round_tokens(0, c)
+        for c in range(CHUNKS):
+            quantise_tokens(0, c)
+        for c in range(CHUNKS):
+            round_tokens(1, c)
+            gather(0, 2 * c, 2 * c + 2)
+            quantise_tokens(1, c)
+
+        w1_codes = {e: w1_first[:, e * PASSES:(e + 1) * PASSES, :] for e in range(2)}
+        w1_mid = streamed([P, 4 * PASSES, 2 * H], U8, "w1_mid")
+        w1_last = streamed([P, 2 * PASSES, 2 * H], U8, "w1_last")
+        w2_codes = streamed([P, E, 2 * N], U8, "w2_codes")
+        for e in range(2, 6):
+            w1_codes[e] = w1_mid[:, (e - 2) * PASSES:(e - 1) * PASSES, :]
+        for e in range(6, 8):
+            w1_codes[e] = w1_last[:, (e - 6) * PASSES:(e - 5) * PASSES, :]
+        load_words(w1_mid[:, 0:2 * PASSES, :], w1_words[2:4])
+        load_words(w1_mid[:, 2 * PASSES:, :], w1_words[4:6])
+        load_words(w1_codes[6], w1_words[6:7])
+        load_words(w1_codes[7], w1_words[7:8])
+        load_words(w2_codes[:, 0:4, :], w2_words[0:4])
+        load_words(w2_codes[:, 4:8, :], w2_words[4:8])
+        gate_sb = [streamed([P, TOP, T], F32, f"gate_sb{m}") for m in range(N_TILES)]
+        for r in range(TOP):
+            nc.sync.dma_start(gate_sb[0][:, r, :], gate[r, 0:P, :])
+        nc.sync.dma_start(gate_sb[1][:], gate[:, P:2 * P, :].rearrange("r n t -> n r t"))
+
+        gather(1, 0, 1)
+        first_layer(0)
+        gather(1, 1, 2)
+        first_layer(1)
+        gather(1, 2, 4)
+        turn(0, 2)
+        first_layer(2)
+        first_layer(3)
+        gather(1, 4, 6)
+        quantise_h(0, 2)
+        first_layer(4)
+        turn(2, 4)
+        first_layer(5)
+        gather(0, 6, 8)
+        gather(1, 6, 8)
+        quantise_h(2, 4)
+        first_layer(6)
+        turn(4, 6)
+        first_layer(7)
+        quantise_h(4, 6)
+        second_layer(0, 0, 4)
+        turn(6, 7, on_vector=True)
+        leave_psum(0, 0, 4, on_vector=True)
+        quantise_h(6, 7)
+        turn(7, 8)
+        second_layer(0, 4, 6)
+        quantise_h(7, 8)
+        second_layer(0, 6, 8)
+        leave_psum(0, 4, 8)
+        second_layer(1, 0, 8)
+        leave_psum(1, 0, 4)
+        leave_psum(1, 4, 8)
+
+        for i, (m, t0, t1) in enumerate(COMBINE_PIECES):
+            terms = [held([P, t1 - t0], F32, f"term{i}_{r}") for r in range(TOP)]
+            for r in range(TOP):
+                picked = y_sb[m][:].indirect(pos_sb[r][:, t0 // LIST_COL:t1 // LIST_COL])
+                nc.vector.tensor_tensor(terms[r][:], picked, gate_sb[m][:, r, t0:t1], ALU.mult)
+            total = held([P, t1 - t0], F32, f"total{i}")
+            nc.vector.tensor_tensor(total[:], terms[0][:], terms[1][:], ALU.add)
+            result = held([P, t1 - t0], F32, f"result{i}")
+            nc.vector.tensor_tensor(result[:], total[:], terms[2][:], ALU.add)
+            nc.sync.dma_start(out[m * P:(m + 1) * P, t0:t1], result[:])

@@ -31,7 +31,10 @@ PAIRS = E // PAIR
 PAIR_SLOTS = PAIR * C
 N_TILES = N // P
 LIST_COL = 16
-COMBINE_PIECES = ((0, 0, 384), (0, 384, 768), (1, 0, 384), (1, 384, 640), (1, 640, 768))
+X_LOADS = ((0, 0, 512), (0, 512, 768), (1, 0, 256), (1, 256, 512), (1, 512, 768))
+TENSOR_PIECES = ((0, 0, 384), (0, 384, 768), (1, 0, 256), (1, 256, 512))
+PSUM_BUFS = {"wide": 4, "turned": 2, "y_first": 2}
+VECTOR_PIECE = (1, 512, 768)
 
 
 def tile_moe_ecr_mlp_gelu_kernel(tc, xT, w1_words, w1_scales, w2_words, w2_scales, gate, offs, pos1, pos2, pos3, out):
@@ -46,12 +49,10 @@ def tile_moe_ecr_mlp_gelu_kernel(tc, xT, w1_words, w1_scales, w2_words, w2_scale
         offs_sb = keep.tile([P, SLOTS // LIST_COL], U16, name="offs_sb")
         pos_sb = [keep.tile([P, T // LIST_COL], U16, name=f"pos_sb{r}") for r in range(TOP)]
         def streamed(shape, dtype, name):
-            return keep.tile(shape, dtype, name=name, tag="streamed", bufs=4, align_bytes=64)
+            return keep.tile(shape, dtype, name=name, tag="streamed", bufs=len(X_LOADS), align_bytes=64)
 
-        x_first = streamed([P, PACK, T], F32, "x_first")
-        x_second = [streamed([P, PACK, TOKEN_CHUNK], F32, f"x_second{c}") for c in range(CHUNKS)]
-        x_raw = [[x_first[:, :, c * TOKEN_CHUNK:(c + 1) * TOKEN_CHUNK] for c in range(CHUNKS)], [t[:] for t in x_second]]
-        x_bf = [[held([P, TOKEN_CHUNK, PACK], BF16, f"x_bf{s}_{c}") for c in range(CHUNKS)] for s in range(PASSES)]
+        x_raw = {(s, t0): streamed([P, PACK, t1 - t0], F32, f"x_raw{s}_{t0}") for s, t0, t1 in X_LOADS}
+        x_bf = [keep.tile([P, T, PACK], BF16, name=f"x_bf{s}", tag=f"x_bf{s}", align_bytes=64) for s in range(PASSES)]
         token_codes = [held([P, T], U32, f"token_codes{s}") for s in range(PASSES)]
         token_scales = [held([P, T], U8, f"token_scales{s}") for s in range(PASSES)]
         w1_plane = [held([P, E // 2 * PASSES, H], U8, f"w1_plane{h}") for h in range(2)]
@@ -59,13 +60,17 @@ def tile_moe_ecr_mlp_gelu_kernel(tc, xT, w1_words, w1_scales, w2_words, w2_scale
         y_sb = [held([P, SLOTS + PAD], F32, f"y_sb{m}") for m in range(N_TILES)]
         identity = held([P, P], F32, "identity")
 
-        nc.gpsimd.memset(w1_plane[0][:].rearrange("p a b -> p (a b)").bitcast(I32), 0)
-        for plane in (w2_plane, w1_plane[1]):
-            nc.vector.memset(plane[:].rearrange("p a b -> p (a b)").bitcast(I32), 0)
-        for plane in token_scales:
-            nc.vector.memset(plane[:].bitcast(I32), 0)
+        def zero(engine, tile_bytes):
+            engine.memset(tile_bytes.rearrange("p a b -> p (a b)").bitcast(I32), 0)
+
+        zero(nc.gpsimd, w1_plane[0][:, 0:4, :])
+        zero(nc.vector, w1_plane[0][:, 4:8, :])
         nc.vector.memset(y_sb[0][:, SLOTS:], 0.0)
         nc.scalar.activation(y_sb[1][:, SLOTS:], y_sb[0][:, SLOTS:], ACT.Gelu_apprx_tanh)
+        for plane in token_scales:
+            nc.vector.memset(plane[:].bitcast(I32), 0)
+        zero(nc.vector, w1_plane[1][:])
+        zero(nc.vector, w2_plane[:])
         make_identity(nc, identity[:])
 
         def x_rows(s):
@@ -79,44 +84,47 @@ def tile_moe_ecr_mlp_gelu_kernel(tc, xT, w1_words, w1_scales, w2_words, w2_scale
         def load_words(dst, words):
             nc.sync.dma_start(dst.bitcast(I32), words.rearrange("e s p b -> p (e s) b").bitcast(I32))
 
-        nc.sync.dma_start(x_first[:], x_rows(0))
-        nc.sync.dma_start(offs_sb[:], offs)
-        for c in range(CHUNKS):
-            nc.sync.dma_start(x_second[c][:], x_rows(1)[:, :, c * TOKEN_CHUNK:(c + 1) * TOKEN_CHUNK])
-        w1_first = held([P, 2 * PASSES, 2 * H], U8, "w1_first")
-        load_words(w1_first[:], w1_words[0:2])
+        for s, t0, t1 in X_LOADS:
+            nc.sync.dma_start(x_raw[s, t0][:], x_rows(s)[:, :, t0:t1])
+            if (s, t1) == (0, T):
+                for dst, entries in zip([offs_sb] + pos_sb, (offs, pos1, pos2, pos3)):
+                    nc.sync.dma_start(dst[:], entries)
         load_plane(w1_plane[0], w1_scales[0:4])
-        load_plane(w2_plane, w2_scales)
+        w1_first = held([P, 4 * PASSES, 2 * H], U8, "w1_first")
+        load_words(w1_first[:, 0:2 * PASSES, :], w1_words[0:2])
+        load_words(w1_first[:, 2 * PASSES:, :], w1_words[2:4])
         load_plane(w1_plane[1], w1_scales[4:8])
-        for r, pos in enumerate((pos1, pos2, pos3)):
-            nc.sync.dma_start(pos_sb[r][:], pos)
-        def round_tokens(s, c):
-            src = x_raw[s][c].rearrange("p j (a i) -> p a j i", i=4)
-            dst = x_bf[s][c][:].rearrange("p (a i) j -> p a j i", i=4)
-            if s == 0 and c < 2:
+        load_plane(w2_plane, w2_scales)
+
+        def round_tokens(s, load, t0, t1, on_vector=False):
+            src = x_raw[s, load][:, :, t0 - load:t1 - load].rearrange("p j (a i) -> p a j i", i=4)
+            dst = x_bf[s][:, t0:t1, :].rearrange("p (a i) j -> p a j i", i=4)
+            if on_vector:
                 nc.vector.tensor_copy(dst, src)
             else:
                 nc.scalar.activation(dst, src, ACT.Copy)
 
-        def quantise_tokens(s, c):
-            cols = slice(c * TOKEN_CHUNK, (c + 1) * TOKEN_CHUNK)
+        def quantise_tokens(s, t0, t1):
             nc.vector.quantize_mx(
-                out=token_codes[s][:, cols].bitcast(FP8X4),
-                scales=token_scales[s][:, cols],
-                in_=x_bf[s][c][:].rearrange("p t j -> p (t j)"),
+                out=token_codes[s][:, t0:t1].bitcast(FP8X4),
+                scales=token_scales[s][:, t0:t1],
+                in_=x_bf[s][:, t0:t1, :].rearrange("p t j -> p (t j)"),
             )
 
         slot_codes, slot_scales, h_rows, turned, h_bf, h_codes, h_scales, y_bank = {}, {}, {}, {}, {}, {}, {}, {}
 
-        def gather(s, e0, e1):
+        def gather(gathered, window, dtype, s, e0, e1, tag):
             entries = offs_sb[:, e0 * C // LIST_COL:e1 * C // LIST_COL]
-            codes = held([P, (e1 - e0) * C], U32, f"slot_codes{s}_{e0}")
-            scales = held([P, (e1 - e0) * C], U8, f"slot_scales{s}_{e0}")
-            nc.vector.tensor_copy(codes[:], token_codes[s][:].indirect(entries))
-            nc.vector.tensor_copy(scales[:], token_scales[s][:].indirect(entries))
+            dst = keep.tile([P, (e1 - e0) * C], dtype, name=f"slots_{tag}", tag=tag, align_bytes=64)
+            nc.vector.tensor_copy(dst[:], window[s][:].indirect(entries))
             for e in range(e0, e1):
-                slot_codes[s, e] = codes[:, (e - e0) * C:(e - e0 + 1) * C]
-                slot_scales[s, e] = scales[:, (e - e0) * C:(e - e0 + 1) * C]
+                gathered[s, e] = dst[:, (e - e0) * C:(e - e0 + 1) * C]
+
+        def gather_codes(s, e0, e1):
+            gather(slot_codes, token_codes, U32, s, e0, e1, f"codes{s}_{e0}")
+
+        def gather_scales(s, e0, e1, tag=None):
+            gather(slot_scales, token_scales, U8, s, e0, e1, tag or f"scales{s}_{e0}")
 
         def first_layer(e):
             a_bank = psum.tile([P, H], F32, name=f"a_bank{e}", tag="wide", bufs=4)
@@ -159,13 +167,11 @@ def tile_moe_ecr_mlp_gelu_kernel(tc, xT, w1_words, w1_scales, w2_words, w2_scale
                 h_codes[e] = codes[:, (e - e0) * C:(e - e0 + 1) * C]
                 h_scales[e] = scales[:, (e - e0) * C:(e - e0 + 1) * C]
 
-        def second_layer(m, e0, e1):
+        def second_layer(m, e0, e1, tag):
+            y_bank[m, e0] = psum.tile([P, (e1 - e0) * C], F32, name=f"y_bank{m}_{e0}", tag=tag, bufs=PSUM_BUFS[tag])
             for e in range(e0, e1):
-                if e % 4 == 0:
-                    tag, bufs = ("y_first", 2) if m == 0 else ("wide", 4)
-                    y_bank[m, e // 4] = psum.tile([P, 4 * C], F32, name=f"y_bank{m}_{e}", tag=tag, bufs=bufs)
                 nc.tensor.matmul_mx(
-                    out=y_bank[m, e // 4][:, (e % 4) * C:(e % 4 + 1) * C],
+                    out=y_bank[m, e0][:, (e - e0) * C:(e - e0 + 1) * C],
                     lhsT=w2_codes[:, e, 2 * P * m:2 * P * (m + 1)].bitcast(FP4X4),
                     lhsT_scale=w2_plane[:, e, P * m:P * (m + 1)],
                     rhs=h_codes[e].bitcast(FP8X4),
@@ -176,31 +182,28 @@ def tile_moe_ecr_mlp_gelu_kernel(tc, xT, w1_words, w1_scales, w2_words, w2_scale
 
         def leave_psum(m, e0, e1, on_vector=False):
             dst = y_sb[m][:, e0 * C:e1 * C]
-            src = y_bank[m, e0 // 4][:, (e0 % 4) * C:(e0 % 4 + e1 - e0) * C]
             if on_vector:
-                nc.vector.tensor_copy(dst, src)
+                nc.vector.tensor_copy(dst, y_bank[m, e0][:])
             else:
-                nc.scalar.copy(dst, src)
+                nc.scalar.copy(dst, y_bank[m, e0][:])
 
-        for c in (2, 0, 1):
-            round_tokens(0, c)
-        for c in range(CHUNKS):
-            quantise_tokens(0, c)
-        for c in range(CHUNKS):
-            round_tokens(1, c)
-            gather(0, 2 * c, 2 * c + 2)
-            quantise_tokens(1, c)
+        round_tokens(0, 0, 0, 512, on_vector=True)
+        round_tokens(0, 512, 512, 640)
+        round_tokens(0, 512, 640, 768, on_vector=True)
+        quantise_tokens(0, 0, 512)
+        quantise_tokens(0, 512, 768)
+        for t0 in (0, 256, 512):
+            round_tokens(1, t0, t0, t0 + 256)
+        gather_codes(0, 0, 4)
+        gather_scales(0, 0, 4)
+        quantise_tokens(1, 0, 512)
+        gather_codes(0, 4, 8)
+        quantise_tokens(1, 512, 768)
 
-        w1_codes = {e: w1_first[:, e * PASSES:(e + 1) * PASSES, :] for e in range(2)}
-        w1_mid = streamed([P, 4 * PASSES, 2 * H], U8, "w1_mid")
-        w1_last = streamed([P, 2 * PASSES, 2 * H], U8, "w1_last")
+        w1_second = streamed([P, 4 * PASSES, 2 * H], U8, "w1_second")
         w2_codes = streamed([P, E, 2 * N], U8, "w2_codes")
-        for e in range(2, 6):
-            w1_codes[e] = w1_mid[:, (e - 2) * PASSES:(e - 1) * PASSES, :]
-        for e in range(6, 8):
-            w1_codes[e] = w1_last[:, (e - 6) * PASSES:(e - 5) * PASSES, :]
-        load_words(w1_mid[:, 0:2 * PASSES, :], w1_words[2:4])
-        load_words(w1_mid[:, 2 * PASSES:, :], w1_words[4:6])
+        w1_codes = {e: (w1_first, w1_second)[e // 4][:, (e % 4) * PASSES:(e % 4 + 1) * PASSES, :] for e in range(E)}
+        load_words(w1_second[:, 0:2 * PASSES, :], w1_words[4:6])
         load_words(w1_codes[6], w1_words[6:7])
         load_words(w1_codes[7], w1_words[7:8])
         load_words(w2_codes[:, 0:4, :], w2_words[0:4])
@@ -210,46 +213,68 @@ def tile_moe_ecr_mlp_gelu_kernel(tc, xT, w1_words, w1_scales, w2_words, w2_scale
             nc.sync.dma_start(gate_sb[0][:, r, :], gate[r, 0:P, :])
         nc.sync.dma_start(gate_sb[1][:], gate[:, P:2 * P, :].rearrange("r n t -> n r t"))
 
-        gather(1, 0, 1)
-        first_layer(0)
-        gather(1, 1, 2)
-        first_layer(1)
-        gather(1, 2, 4)
+        for e0, e1 in ((0, 1), (1, 2), (2, 4)):
+            gather_codes(1, e0, e1)
+            gather_scales(1, e0, e1)
+        gather_scales(0, 4, 8, tag="x_bf1")
+        gather_codes(1, 4, 6)
+        gather_scales(1, 4, 6)
+        gather_scales(1, 6, 8)
+        gather_codes(1, 6, 7)
+        gather_codes(1, 7, 8)
+
+        for e in range(4):
+            first_layer(e)
         turn(0, 2)
-        first_layer(2)
-        first_layer(3)
-        gather(1, 4, 6)
-        quantise_h(0, 2)
-        first_layer(4)
         turn(2, 4)
-        first_layer(5)
-        gather(0, 6, 8)
-        gather(1, 6, 8)
+        for e in range(4, 8):
+            first_layer(e)
+        quantise_h(0, 2)
         quantise_h(2, 4)
-        first_layer(6)
-        turn(4, 6)
-        first_layer(7)
-        quantise_h(4, 6)
-        second_layer(0, 0, 4)
-        turn(6, 7, on_vector=True)
-        leave_psum(0, 0, 4, on_vector=True)
-        quantise_h(6, 7)
+        turn(4, 6, on_vector=True)
+        turn(6, 7)
+        second_layer(0, 0, 4, "y_first")
         turn(7, 8)
-        second_layer(0, 4, 6)
+        quantise_h(4, 6)
+        quantise_h(6, 7)
         quantise_h(7, 8)
-        second_layer(0, 6, 8)
-        leave_psum(0, 4, 8)
-        second_layer(1, 0, 8)
+        leave_psum(0, 0, 4)
+        second_layer(0, 4, 6, "y_first")
+        leave_psum(0, 4, 6, on_vector=True)
+        second_layer(0, 6, 8, "wide")
+        leave_psum(0, 6, 8)
+        second_layer(1, 0, 4, "wide")
+        second_layer(1, 4, 8, "wide")
         leave_psum(1, 0, 4)
         leave_psum(1, 4, 8)
 
-        for i, (m, t0, t1) in enumerate(COMBINE_PIECES):
-            terms = [held([P, t1 - t0], F32, f"term{i}_{r}") for r in range(TOP)]
+        def weighted_terms(m, t0, t1):
+            terms = [held([P, t1 - t0], F32, f"term{m}_{t0}_{r}") for r in range(TOP)]
             for r in range(TOP):
                 picked = y_sb[m][:].indirect(pos_sb[r][:, t0 // LIST_COL:t1 // LIST_COL])
                 nc.vector.tensor_tensor(terms[r][:], picked, gate_sb[m][:, r, t0:t1], ALU.mult)
-            total = held([P, t1 - t0], F32, f"total{i}")
-            nc.vector.tensor_tensor(total[:], terms[0][:], terms[1][:], ALU.add)
-            result = held([P, t1 - t0], F32, f"result{i}")
-            nc.vector.tensor_tensor(result[:], total[:], terms[2][:], ALU.add)
+            return terms
+
+        for m, t0, t1 in TENSOR_PIECES:
+            terms = weighted_terms(m, t0, t1)
+            blocks = [slice(b, b + P) for b in range(0, t1 - t0, P)]
+            summed = psum.tile([P, t1 - t0], F32, name=f"summed{m}_{t0}", tag="turned", bufs=2)
+            for cols in blocks:
+                for r in range(TOP):
+                    nc.tensor.matmul(summed[:, cols], terms[r][:, cols], identity[:], start=(r == 0), stop=(r == TOP - 1), is_transpose=True)
+            by_token = held([P, t1 - t0], F32, f"by_token{m}_{t0}")
+            nc.scalar.copy(by_token[:], summed[:])
+            back = psum.tile([P, t1 - t0], F32, name=f"back{m}_{t0}", tag="y_first", bufs=2)
+            for cols in blocks:
+                nc.tensor.transpose(back[:, cols], by_token[:, cols], identity[:])
+            result = held([P, t1 - t0], F32, f"result{m}_{t0}")
+            nc.scalar.copy(result[:], back[:])
             nc.sync.dma_start(out[m * P:(m + 1) * P, t0:t1], result[:])
+
+        m, t0, t1 = VECTOR_PIECE
+        terms = weighted_terms(m, t0, t1)
+        total = held([P, t1 - t0], F32, "total")
+        nc.vector.tensor_tensor(total[:], terms[0][:], terms[1][:], ALU.add)
+        result = held([P, t1 - t0], F32, "result")
+        nc.vector.tensor_tensor(result[:], total[:], terms[2][:], ALU.add)
+        nc.sync.dma_start(out[m * P:(m + 1) * P, t0:t1], result[:])

from contextlib import ExitStack

import concourse.mybir as mybir
from concourse.masks import make_identity

K, T, E, C, H, N = 1024, 768, 8, 128, 512, 256
TOP = 3
PAD = 64
SLOTS = E * C
FLOPS = 2 * SLOTS * (K * H + H * N)

F32 = mybir.dt.float32
BF16 = mybir.dt.bfloat16
I32 = mybir.dt.int32
U32 = mybir.dt.uint32
U16 = mybir.dt.uint16
U8 = mybir.dt.uint8
FP8X4 = mybir.dt.float8_e4m3fn_x4
FP4X4 = mybir.dt.float4_e2m1fn_x4
ACT = mybir.ActivationFunctionType
ALU = mybir.AluOpType

P = 128
PACK = 4
K_PASS = P * PACK
PASSES = K // K_PASS
TOKEN_CHUNK = 256
CHUNKS = T // TOKEN_CHUNK
PAIR = 2
PAIRS = E // PAIR
PAIR_SLOTS = PAIR * C
N_TILES = N // P
LIST_COL = 16
X_LOADS = ((0, 0, 512), (0, 512, 768), (1, 0, 256), (1, 256, 512), (1, 512, 768))
TENSOR_PIECES = ((0, 0, 384), (0, 384, 768), (1, 0, 256), (1, 256, 512))
PSUM_BUFS = {"wide": 4, "turned": 2, "y_first": 2}
VECTOR_PIECE = (1, 512, 768)


def tile_moe_ecr_mlp_gelu_kernel(tc, xT, w1_words, w1_scales, w2_words, w2_scales, gate, offs, pos1, pos2, pos3, out):
    nc = tc.nc
    with ExitStack() as ctx:
        keep = ctx.enter_context(tc.tile_pool(name="keep", bufs=1))
        psum = ctx.enter_context(tc.psum_pool(name="psum", bufs=1))

        def held(shape, dtype, name):
            return keep.tile(shape, dtype, name=name, align_bytes=64)

        offs_sb = keep.tile([P, SLOTS // LIST_COL], U16, name="offs_sb")
        pos_sb = [keep.tile([P, T // LIST_COL], U16, name=f"pos_sb{r}") for r in range(TOP)]
        def streamed(shape, dtype, name):
            return keep.tile(shape, dtype, name=name, tag="streamed", bufs=len(X_LOADS), align_bytes=64)

        x_raw = {(s, t0): streamed([P, PACK, t1 - t0], F32, f"x_raw{s}_{t0}") for s, t0, t1 in X_LOADS}
        x_bf = [keep.tile([P, T, PACK], BF16, name=f"x_bf{s}", tag=f"x_bf{s}", align_bytes=64) for s in range(PASSES)]
        token_codes = [held([P, T], U32, f"token_codes{s}") for s in range(PASSES)]
        token_scales = [held([P, T], U8, f"token_scales{s}") for s in range(PASSES)]
        w1_plane = [held([P, E // 2 * PASSES, H], U8, f"w1_plane{h}") for h in range(2)]
        w2_plane = held([P, E, N], U8, "w2_plane")
        y_sb = [held([P, SLOTS + PAD], F32, f"y_sb{m}") for m in range(N_TILES)]
        identity = held([P, P], F32, "identity")

        def zero(engine, tile_bytes):
            engine.memset(tile_bytes.rearrange("p a b -> p (a b)").bitcast(I32), 0)

        zero(nc.gpsimd, w1_plane[0][:, 0:4, :])
        zero(nc.vector, w1_plane[0][:, 4:8, :])
        nc.vector.memset(y_sb[0][:, SLOTS:], 0.0)
        nc.scalar.activation(y_sb[1][:, SLOTS:], y_sb[0][:, SLOTS:], ACT.Gelu_apprx_tanh)
        for plane in token_scales:
            nc.vector.memset(plane[:].bitcast(I32), 0)
        zero(nc.vector, w1_plane[1][:])
        zero(nc.vector, w2_plane[:])
        make_identity(nc, identity[:])

        def x_rows(s):
            return xT[s * K_PASS:(s + 1) * K_PASS, :].rearrange("(p j) t -> p j t", j=PACK)

        def load_plane(plane, scales):
            rows = scales.rearrange("e s (q r) i -> r q (e s) i", r=4)
            for r in range(4):
                nc.sync.dma_start(plane[r:P:32, :, :].bitcast(I32), rows[r].bitcast(I32))

        def load_words(dst, words):
            nc.sync.dma_start(dst.bitcast(I32), words.rearrange("e s p b -> p (e s) b").bitcast(I32))

        for s, t0, t1 in X_LOADS:
            nc.sync.dma_start(x_raw[s, t0][:], x_rows(s)[:, :, t0:t1])
            if (s, t1) == (0, T):
                for dst, entries in zip([offs_sb] + pos_sb, (offs, pos1, pos2, pos3)):
                    nc.sync.dma_start(dst[:], entries)
        load_plane(w1_plane[0], w1_scales[0:4])
        w1_first = held([P, 4 * PASSES, 2 * H], U8, "w1_first")
        load_words(w1_first[:, 0:2 * PASSES, :], w1_words[0:2])
        load_words(w1_first[:, 2 * PASSES:, :], w1_words[2:4])
        load_plane(w1_plane[1], w1_scales[4:8])
        load_plane(w2_plane, w2_scales)

        def round_tokens(s, load, t0, t1, on_vector=False):
            src = x_raw[s, load][:, :, t0 - load:t1 - load].rearrange("p j (a i) -> p a j i", i=4)
            dst = x_bf[s][:, t0:t1, :].rearrange("p (a i) j -> p a j i", i=4)
            if on_vector:
                nc.vector.tensor_copy(dst, src)
            else:
                nc.scalar.activation(dst, src, ACT.Copy)

        def quantise_tokens(s, t0, t1):
            nc.vector.quantize_mx(
                out=token_codes[s][:, t0:t1].bitcast(FP8X4),
                scales=token_scales[s][:, t0:t1],
                in_=x_bf[s][:, t0:t1, :].rearrange("p t j -> p (t j)"),
            )

        slot_codes, slot_scales, h_rows, turned, h_bf, h_codes, h_scales, y_bank = {}, {}, {}, {}, {}, {}, {}, {}

        def gather(gathered, window, dtype, s, e0, e1, tag):
            entries = offs_sb[:, e0 * C // LIST_COL:e1 * C // LIST_COL]
            dst = keep.tile([P, (e1 - e0) * C], dtype, name=f"slots_{tag}", tag=tag, align_bytes=64)
            nc.vector.tensor_copy(dst[:], window[s][:].indirect(entries))
            for e in range(e0, e1):
                gathered[s, e] = dst[:, (e - e0) * C:(e - e0 + 1) * C]

        def gather_codes(s, e0, e1):
            gather(slot_codes, token_codes, U32, s, e0, e1, f"codes{s}_{e0}")

        def gather_scales(s, e0, e1, tag=None):
            gather(slot_scales, token_scales, U8, s, e0, e1, tag or f"scales{s}_{e0}")

        def first_layer(e):
            a_bank = psum.tile([P, H], F32, name=f"a_bank{e}", tag="wide", bufs=4)
            for s in range(PASSES):
                nc.tensor.matmul_mx(
                    out=a_bank[:],
                    lhsT=slot_codes[s, e].bitcast(FP8X4),
                    lhsT_scale=slot_scales[s, e],
                    rhs=w1_codes[e][:, s, :].bitcast(FP4X4),
                    rhs_scale=w1_plane[e // 4][:, (e % 4) * PASSES + s, :],
                    start=(s == 0),
                    stop=(s == PASSES - 1),
                )
            h_rows[e] = held([P, H], BF16, f"h_rows{e}")
            nc.scalar.activation(
                h_rows[e][:].rearrange("c (u m d) -> c u m d", u=2, d=2),
                a_bank[:].rearrange("c (m u d) -> c u m d", u=2, d=2),
                ACT.Gelu_apprx_tanh,
            )

        def turn(e0, e1, on_vector=False):
            bank = psum.tile([P, e1 - e0, 2, C], F32, name=f"turned{e0}", tag="turned", bufs=2)
            for e in range(e0, e1):
                h_words = h_rows[e][:].bitcast(F32)
                for u in range(2):
                    nc.tensor.transpose(bank[:, e - e0, u, :], h_words[:, u * P:(u + 1) * P], identity[:])
            h_bf[e0] = held([P, (e1 - e0) * C * PACK], BF16, f"h_bf{e0}")
            dst = h_bf[e0][:].bitcast(F32).rearrange("p (j c u) -> p j c u", j=e1 - e0, u=2)
            src = bank[:].rearrange("p j u c -> p j c u")
            if on_vector:
                nc.vector.tensor_copy(dst, src)
            else:
                nc.scalar.copy(dst, src)

        def quantise_h(e0, e1):
            codes = held([P, (e1 - e0) * C], U32, f"h_codes{e0}")
            scales = held([P, (e1 - e0) * C], U8, f"h_scales{e0}")
            nc.vector.quantize_mx(out=codes[:].bitcast(FP8X4), scales=scales[:], in_=h_bf[e0][:])
            for e in range(e0, e1):
                h_codes[e] = codes[:, (e - e0) * C:(e - e0 + 1) * C]
                h_scales[e] = scales[:, (e - e0) * C:(e - e0 + 1) * C]

        def second_layer(m, e0, e1, tag):
            y_bank[m, e0] = psum.tile([P, (e1 - e0) * C], F32, name=f"y_bank{m}_{e0}", tag=tag, bufs=PSUM_BUFS[tag])
            for e in range(e0, e1):
                nc.tensor.matmul_mx(
                    out=y_bank[m, e0][:, (e - e0) * C:(e - e0 + 1) * C],
                    lhsT=w2_codes[:, e, 2 * P * m:2 * P * (m + 1)].bitcast(FP4X4),
                    lhsT_scale=w2_plane[:, e, P * m:P * (m + 1)],
                    rhs=h_codes[e].bitcast(FP8X4),
                    rhs_scale=h_scales[e],
                    start=True,
                    stop=True,
                )

        def leave_psum(m, e0, e1, on_vector=False):
            dst = y_sb[m][:, e0 * C:e1 * C]
            if on_vector:
                nc.vector.tensor_copy(dst, y_bank[m, e0][:])
            else:
                nc.scalar.copy(dst, y_bank[m, e0][:])

        round_tokens(0, 0, 0, 512, on_vector=True)
        round_tokens(0, 512, 512, 640)
        round_tokens(0, 512, 640, 768, on_vector=True)
        quantise_tokens(0, 0, 512)
        quantise_tokens(0, 512, 768)
        for t0 in (0, 256, 512):
            round_tokens(1, t0, t0, t0 + 256)
        gather_codes(0, 0, 4)
        gather_scales(0, 0, 4)
        quantise_tokens(1, 0, 512)
        gather_codes(0, 4, 8)
        quantise_tokens(1, 512, 768)

        w1_second = streamed([P, 4 * PASSES, 2 * H], U8, "w1_second")
        w2_codes = streamed([P, E, 2 * N], U8, "w2_codes")
        w1_codes = {e: (w1_first, w1_second)[e // 4][:, (e % 4) * PASSES:(e % 4 + 1) * PASSES, :] for e in range(E)}
        load_words(w1_second[:, 0:2 * PASSES, :], w1_words[4:6])
        load_words(w1_codes[6], w1_words[6:7])
        load_words(w1_codes[7], w1_words[7:8])
        load_words(w2_codes[:, 0:4, :], w2_words[0:4])
        load_words(w2_codes[:, 4:8, :], w2_words[4:8])
        gate_sb = [streamed([P, TOP, T], F32, f"gate_sb{m}") for m in range(N_TILES)]
        for r in range(TOP):
            nc.sync.dma_start(gate_sb[0][:, r, :], gate[r, 0:P, :])
        nc.sync.dma_start(gate_sb[1][:], gate[:, P:2 * P, :].rearrange("r n t -> n r t"))

        for e0, e1 in ((0, 1), (1, 2), (2, 4)):
            gather_codes(1, e0, e1)
            gather_scales(1, e0, e1)
        gather_scales(0, 4, 8, tag="x_bf1")
        gather_codes(1, 4, 6)
        gather_scales(1, 4, 6)
        gather_scales(1, 6, 8)
        gather_codes(1, 6, 7)
        gather_codes(1, 7, 8)

        for e in range(4):
            first_layer(e)
        turn(0, 2)
        turn(2, 4)
        for e in range(4, 8):
            first_layer(e)
        quantise_h(0, 2)
        quantise_h(2, 4)
        turn(4, 6, on_vector=True)
        turn(6, 7)
        second_layer(0, 0, 4, "y_first")
        turn(7, 8)
        quantise_h(4, 6)
        quantise_h(6, 7)
        quantise_h(7, 8)
        leave_psum(0, 0, 4)
        second_layer(0, 4, 6, "y_first")
        leave_psum(0, 4, 6, on_vector=True)
        second_layer(0, 6, 8, "wide")
        leave_psum(0, 6, 8)
        second_layer(1, 0, 4, "wide")
        second_layer(1, 4, 8, "wide")
        leave_psum(1, 0, 4)
        leave_psum(1, 4, 8)

        def weighted_terms(m, t0, t1):
            terms = [held([P, t1 - t0], F32, f"term{m}_{t0}_{r}") for r in range(TOP)]
            for r in range(TOP):
                picked = y_sb[m][:].indirect(pos_sb[r][:, t0 // LIST_COL:t1 // LIST_COL])
                nc.vector.tensor_tensor(terms[r][:], picked, gate_sb[m][:, r, t0:t1], ALU.mult)
            return terms

        for m, t0, t1 in TENSOR_PIECES:
            terms = weighted_terms(m, t0, t1)
            blocks = [slice(b, b + P) for b in range(0, t1 - t0, P)]
            summed = psum.tile([P, t1 - t0], F32, name=f"summed{m}_{t0}", tag="turned", bufs=2)
            for cols in blocks:
                for r in range(TOP):
                    nc.tensor.matmul(summed[:, cols], terms[r][:, cols], identity[:], start=(r == 0), stop=(r == TOP - 1), is_transpose=True)
            by_token = held([P, t1 - t0], F32, f"by_token{m}_{t0}")
            nc.scalar.copy(by_token[:], summed[:])
            back = psum.tile([P, t1 - t0], F32, name=f"back{m}_{t0}", tag="y_first", bufs=2)
            for cols in blocks:
                nc.tensor.transpose(back[:, cols], by_token[:, cols], identity[:])
            result = held([P, t1 - t0], F32, f"result{m}_{t0}")
            nc.scalar.copy(result[:], back[:])
            nc.sync.dma_start(out[m * P:(m + 1) * P, t0:t1], result[:])

        m, t0, t1 = VECTOR_PIECE
        terms = weighted_terms(m, t0, t1)
        total = held([P, t1 - t0], F32, "total")
        nc.vector.tensor_tensor(total[:], terms[0][:], terms[1][:], ALU.add)
        result = held([P, t1 - t0], F32, "result")
        nc.vector.tensor_tensor(result[:], total[:], terms[2][:], ALU.add)
        nc.sync.dma_start(out[m * P:(m + 1) * P, t0:t1], result[:])
